import numpy as np
CORES = [3,11,19,27,35,43,51,59,67,75,83,91]
N = 12
ROOT = 7
def setup_inputs(rng):
    return {"x": rng.standard_normal((N, 128, N * 256), dtype=np.float32)}
def reference(x):
    return {"y": np.stack([x[ROOT][:, r * 256:(r + 1) * 256] for r in range(N)])}

@@ -1,0 +1,95 @@
+from concourse.bass import DstId, RemoteDMATransfer
+
+W = 256
+ROOT_RANK = 7
+HELP_A, HELP_B = 62, 63
+
+DIRECT = [8, 9, 10, 11, 6]
+SLOT = {b: i for i, b in enumerate(DIRECT)}
+
+SCRATCH = {
+    "sb": ("sbuf", [128, 6 * W], "float32"),
+    "st": ("dram", [len(DIRECT), 128, W], "float32"),
+    "land": ("dram", [128, W], "float32"),
+}
+SEMAPHORES = ["l0", "l1", "p0", "p1", "p2", "sent", "hand0", "hand1", "arrived", "stored", "go", "own"]
+
+LO4, HI4, OFF8, ALL16 = 0x000F, 0x00F0, 0x00FF, 0xFFFF
+
+ARRIVE = {0: 4, 1: 4, 2: 4, 3: 4, 4: 4, 5: 4, 8: 4, 9: 4, 10: 4, 11: 4, 6: 8}
+
+
+def rank_program(g, core, T, topo):
+    S = T.sem
+    sy, sc = g.sync, g.scalar
+    root = T.cores[ROOT_RANK]
+
+    def cols(b, n=1):
+        return slice(b * W, (b + n) * W)
+
+    def xfer(src, block, mask):
+        rid, pid, _ = topo.addr(T.cores[block])
+        return RemoteDMATransfer(dst_ids=[DstId(rid=rid, pnc=pid)], dma_engine_mask=mask, remote_sem=S.arrived,
+                                 src=src, dst=T.land[:])
+
+    def pair(src_of, even, odd):
+        g.remote_dma_fused([xfer(src_of(even), even, LO4), xfer(src_of(odd), odd, HI4)], local_sem=S.sent)
+
+    def hand(helper, b, n, sem):
+        rid, pid, _ = topo.addr(helper)
+        g.remote_dma(out_ap=T.sb[:, cols(b, n)], in_ap=T.sb[:, cols(b, n)], remote_sem=sem, local_sem=S.sent,
+                     pid=pid, routing_id=rid, dma_engine_mask=ALL16)
+
+    if core == root:
+        sy.dma_start(T.sb[:, cols(0, 2)], T.x[:, cols(0, 2)]).then_inc(S.l0, 16)
+        sc.dma_start(T.sb[:, cols(2, 4)], T.x[:, cols(2, 4)]).then_inc(S.l1, 16)
+        sy.dma_start(T.st[SLOT[8]], T.x[:, cols(8)]).then_inc(S.p0, 16)
+        sc.dma_start(T.st[SLOT[9]], T.x[:, cols(9)]).then_inc(S.p0, 16)
+        sy.dma_start(T.st[SLOT[10]], T.x[:, cols(10)]).then_inc(S.p1, 16)
+        sc.dma_start(T.st[SLOT[11]], T.x[:, cols(11)]).then_inc(S.p1, 16)
+        sy.dma_start(T.st[SLOT[6]], T.x[:, cols(6)]).then_inc(S.p2, 16)
+
+        g.wait_ge(S.l0, 16)
+        hand(HELP_A, 0, 2, S.hand0)
+        g.wait_ge(S.l1, 16)
+        hand(HELP_B, 2, 2, S.hand0)
+        hand(HELP_A, 4, 2, S.hand1)
+
+        def slot(b):
+            return T.st[SLOT[b]]
+        g.wait_ge(S.p0, 32)
+        pair(slot, 8, 9)
+        g.wait_ge(S.p1, 32)
+        pair(slot, 10, 11)
+        g.wait_ge(S.p2, 16)
+        rid, pid, _ = topo.addr(T.cores[6])
+        g.remote_dma(out_ap=T.land[:], in_ap=slot(6), remote_sem=S.arrived, local_sem=S.sent,
+                     pid=pid, routing_id=rid, dma_engine_mask=OFF8)
+        g.sem_inc(S.go, 1)
+
+        sc.wait_ge(S.go, 1)
+        sc.dma_start(T.y[:], T.x[:, cols(ROOT_RANK)]).then_inc(S.own, 16)
+        sc.wait_ge(S.own, 16)
+        g.wait_ge(S.sent, 3 * 16 + 3 * 8)
+        return
+
+    if core in (HELP_A, HELP_B):
+        def part(b):
+            return T.sb[:, cols(b)]
+        first = 0 if core == HELP_A else 2
+        g.wait_ge(S.hand0, 16)
+        pair(part, first, first + 1)
+        if core == HELP_A:
+            g.wait_ge(S.hand1, 16)
+            pair(part, 4, 5)
+            g.wait_ge(S.sent, 16)
+        else:
+            g.wait_ge(S.sent, 8)
+        return
+
+    rank = T.rank_of(core)
+    if rank is None:
+        return
+    sy.wait_ge(S.arrived, ARRIVE[rank])
+    sy.dma_start(T.y[:], T.land[:]).then_inc(S.stored, 16)
+    sy.wait_ge(S.stored, 16)

@@ -15,7 +15,6 @@ SCRATCH = {
 SEMAPHORES = ["l0", "l1", "p0", "p1", "p2", "sent", "hand0", "hand1", "arrived", "stored", "go", "own"]
 
 LO4, HI4, OFF8, ALL16 = 0x000F, 0x00F0, 0x00FF, 0xFFFF
-
 ARRIVE = {0: 4, 1: 4, 2: 4, 3: 4, 4: 4, 5: 4, 8: 4, 9: 4, 10: 4, 11: 4, 6: 8}
 
 
@@ -43,6 +42,8 @@ def rank_program(g, core, T, topo):
     if core == root:
         sy.dma_start(T.sb[:, cols(0, 2)], T.x[:, cols(0, 2)]).then_inc(S.l0, 16)
         sc.dma_start(T.sb[:, cols(2, 4)], T.x[:, cols(2, 4)]).then_inc(S.l1, 16)
+        sy.wait_ge(S.l0, 16)
+        sc.wait_ge(S.l0, 16)
         sy.dma_start(T.st[SLOT[8]], T.x[:, cols(8)]).then_inc(S.p0, 16)
         sc.dma_start(T.st[SLOT[9]], T.x[:, cols(9)]).then_inc(S.p0, 16)
         sy.dma_start(T.st[SLOT[10]], T.x[:, cols(10)]).then_inc(S.p1, 16)
@@ -62,9 +63,7 @@ def rank_program(g, core, T, topo):
         g.wait_ge(S.p1, 32)
         pair(slot, 10, 11)
         g.wait_ge(S.p2, 16)
-        rid, pid, _ = topo.addr(T.cores[6])
-        g.remote_dma(out_ap=T.land[:], in_ap=slot(6), remote_sem=S.arrived, local_sem=S.sent,
-                     pid=pid, routing_id=rid, dma_engine_mask=OFF8)
+        g.remote_dma_fused([xfer(slot(6), 6, OFF8)], local_sem=S.sent)
         g.sem_inc(S.go, 1)
 
         sc.wait_ge(S.go, 1)

from concourse.bass import DstId, RemoteDMATransfer

W = 256
ROOT_RANK = 7
HELP_A, HELP_B = 62, 63

DIRECT = [8, 9, 10, 11, 6]
SLOT = {b: i for i, b in enumerate(DIRECT)}

SCRATCH = {
    "sb": ("sbuf", [128, 6 * W], "float32"),
    "st": ("dram", [len(DIRECT), 128, W], "float32"),
    "land": ("dram", [128, W], "float32"),
}
SEMAPHORES = ["l0", "l1", "p0", "p1", "p2", "sent", "hand0", "hand1", "arrived", "stored", "go", "own"]

LO4, HI4, OFF8, ALL16 = 0x000F, 0x00F0, 0x00FF, 0xFFFF
ARRIVE = {0: 4, 1: 4, 2: 4, 3: 4, 4: 4, 5: 4, 8: 4, 9: 4, 10: 4, 11: 4, 6: 8}


def rank_program(g, core, T, topo):
    S = T.sem
    sy, sc = g.sync, g.scalar
    root = T.cores[ROOT_RANK]

    def cols(b, n=1):
        return slice(b * W, (b + n) * W)

    def xfer(src, block, mask):
        rid, pid, _ = topo.addr(T.cores[block])
        return RemoteDMATransfer(dst_ids=[DstId(rid=rid, pnc=pid)], dma_engine_mask=mask, remote_sem=S.arrived,
                                 src=src, dst=T.land[:])

    def pair(src_of, even, odd):
        g.remote_dma_fused([xfer(src_of(even), even, LO4), xfer(src_of(odd), odd, HI4)], local_sem=S.sent)

    def hand(helper, b, n, sem):
        rid, pid, _ = topo.addr(helper)
        g.remote_dma(out_ap=T.sb[:, cols(b, n)], in_ap=T.sb[:, cols(b, n)], remote_sem=sem, local_sem=S.sent,
                     pid=pid, routing_id=rid, dma_engine_mask=ALL16)

    if core == root:
        sy.dma_start(T.sb[:, cols(0, 2)], T.x[:, cols(0, 2)]).then_inc(S.l0, 16)
        sc.dma_start(T.sb[:, cols(2, 4)], T.x[:, cols(2, 4)]).then_inc(S.l1, 16)
        sy.wait_ge(S.l0, 16)
        sc.wait_ge(S.l0, 16)
        sy.dma_start(T.st[SLOT[8]], T.x[:, cols(8)]).then_inc(S.p0, 16)
        sc.dma_start(T.st[SLOT[9]], T.x[:, cols(9)]).then_inc(S.p0, 16)
        sy.dma_start(T.st[SLOT[10]], T.x[:, cols(10)]).then_inc(S.p1, 16)
        sc.dma_start(T.st[SLOT[11]], T.x[:, cols(11)]).then_inc(S.p1, 16)
        sy.dma_start(T.st[SLOT[6]], T.x[:, cols(6)]).then_inc(S.p2, 16)

        g.wait_ge(S.l0, 16)
        hand(HELP_A, 0, 2, S.hand0)
        g.wait_ge(S.l1, 16)
        hand(HELP_B, 2, 2, S.hand0)
        hand(HELP_A, 4, 2, S.hand1)

        def slot(b):
            return T.st[SLOT[b]]
        g.wait_ge(S.p0, 32)
        pair(slot, 8, 9)
        g.wait_ge(S.p1, 32)
        pair(slot, 10, 11)
        g.wait_ge(S.p2, 16)
        g.remote_dma_fused([xfer(slot(6), 6, OFF8)], local_sem=S.sent)
        g.sem_inc(S.go, 1)

        sc.wait_ge(S.go, 1)
        sc.dma_start(T.y[:], T.x[:, cols(ROOT_RANK)]).then_inc(S.own, 16)
        sc.wait_ge(S.own, 16)
        g.wait_ge(S.sent, 3 * 16 + 3 * 8)
        return

    if core in (HELP_A, HELP_B):
        def part(b):
            return T.sb[:, cols(b)]
        first = 0 if core == HELP_A else 2
        g.wait_ge(S.hand0, 16)
        pair(part, first, first + 1)
        if core == HELP_A:
            g.wait_ge(S.hand1, 16)
            pair(part, 4, 5)
            g.wait_ge(S.sent, 16)
        else:
            g.wait_ge(S.sent, 8)
        return

    rank = T.rank_of(core)
    if rank is None:
        return
    sy.wait_ge(S.arrived, ARRIVE[rank])
    sy.dma_start(T.y[:], T.land[:]).then_inc(S.stored, 16)
    sy.wait_ge(S.stored, 16)
